import numpy as np
import ml_dtypes


def mxq(x, axis, fmt="e4m3"):
    dtype, down = {"e4m3": (ml_dtypes.float8_e4m3fn, 7), "e5m2": (ml_dtypes.float8_e5m2, 14)}[fmt]
    v = np.moveaxis(np.asarray(x, np.float32).astype(ml_dtypes.bfloat16).astype(np.float64), axis, -1)
    blocks = v.reshape(v.shape[:-1] + (-1, 32))
    amax = np.abs(blocks).max(-1, keepdims=True)
    byte = np.maximum(np.where(amax > 0, np.frexp(amax)[1] - 1 + 127, 0) - down, 1)
    scale = np.exp2(byte - 127.0)
    codes = (blocks / scale).astype(np.float32).astype(dtype).astype(np.float64)
    return np.moveaxis((codes * scale).reshape(v.shape), -1, axis)


WIDE = False


def mx_kscale(k):
    if not WIDE:
        return np.ones(k)
    levels = np.array([10, -10, 5, -5, 0])
    if k % 512:
        return np.exp2(np.random.permutation(np.resize(levels, k // 32))).repeat(32)
    a = np.empty((k // 512, 16))
    for p in range(k // 512):
        a[p, :8] = np.random.permutation(np.resize(levels, 8))
        for g in range(8):
            far = levels[np.abs(levels - a[p, g]) >= 10]
            a[p, g + 8] = far[np.random.randint(len(far))]
    return np.exp2(a.ravel()).repeat(32)


def f64(x):
    return np.asarray(x).astype(np.float64)


def striped(idx):
    return np.tile(np.asarray(idx).reshape(-1, 16).T, (8, 1)).astype(np.uint16)


def unstriped(offs):
    return offs[:16].T.reshape(-1).astype(np.int64)


E2M1 = np.array([0.0, 0.5, 1.0, 1.5, 2.0, 3.0, 4.0, 6.0, -0.0, -0.5, -1.0, -1.5, -2.0, -3.0, -4.0, -6.0])


def pack_weight(w, fmt):
    k, n = w.shape
    w = f64(np.asarray(w, np.float32).astype(ml_dtypes.bfloat16)).reshape(k // 32, 32, n)
    amax = np.abs(w).max(1)
    if fmt == "e4m3":
        byte = np.frexp(amax)[1] - 1 + 127 - 7
    else:
        mant, ex = np.frexp(amax / 6.0)
        byte = np.where(mant > 0.5, ex, ex - 1) + 127
    byte = np.clip(np.where(amax > 0, byte, 1), 1, 254)
    scaled = (w * np.exp2(127.0 - byte)[:, None, :]).reshape(k, n).astype(np.float32)
    by_word = np.ascontiguousarray(scaled.reshape(k // 512, 128, 4, n).transpose(0, 1, 3, 2))
    if fmt == "e4m3":
        words = by_word.astype(ml_dtypes.float8_e4m3fn).view(np.uint8)
    else:
        c = by_word.astype(ml_dtypes.float4_e2m1fn).view(np.uint8) & 0xF
        words = (c[..., 0::2] | (c[..., 1::2] << 4)).reshape(k // 512, 128, 2 * n)
    return np.ascontiguousarray(words), np.ascontiguousarray(byte.astype(np.uint8).reshape(k // 512, 16, n))


def unpack_weight(words, scales, fmt):
    g, _, n = scales.shape
    words = np.ascontiguousarray(words).reshape(g, 128, n, -1)
    if fmt == "e4m3":
        vals = words.view(ml_dtypes.float8_e4m3fn).astype(np.float64)
    else:
        nib = np.empty((g, 128, n, 4), np.uint8)
        nib[..., 0::2] = words & 0xF
        nib[..., 1::2] = words >> 4
        vals = E2M1[nib]
    vals = vals * np.repeat(np.exp2(scales.astype(np.float64) - 127.0), 8, axis=1)[..., None]
    return vals.transpose(0, 1, 3, 2).reshape(g * 512, n)


def sigmoid(v):
    return 1.0 / (1.0 + np.exp(-v))


D, T, U, I, J = 512, 1024, 1024, 256, 512


def setup_inputs():
    n = np.random.standard_normal
    idx = np.random.permutation(T)[:I]
    idx2 = np.random.permutation(U)[:J]
    fd = mx_kscale(D)
    tabbp = pack_weight(n((D, U)) / fd[:, None], "e4m3")
    return {
        "taba": (n((D, T)) * 1 / np.sqrt(D) * fd[:, None]).astype(np.float32),
        "tabb_words": tabbp[0],
        "tabb_scales": tabbp[1],
        "steep": (np.random.uniform(0.7, 2.0, (I, 1))).astype(np.float32),
        "bias": (np.random.uniform(-0.7, 0.7, (1, J))).astype(np.float32),
        "degree": (np.random.uniform(0.0, 1.0, (I, J))).astype(np.float32),
        "pw": (np.random.uniform(0.5, 3.0, (1, J))).astype(np.float32),
        "old": (0.3 * n((I, J))).astype(np.float32),
        "offs": striped(idx),
        "offs2": striped(idx2),
    }


def reference(taba, tabb_words, tabb_scales, steep, bias, degree, pw, old, offs, offs2):
    idx = unstriped(offs)
    idx2 = unstriped(offs2)
    tabbu = unpack_weight(tabb_words, tabb_scales, "e4m3")
    tabaidxq = mxq(f64(taba)[:, idx], 0, "e4m3")
    tabbidx2g = tabbu[:, idx2]
    s = tabaidxq.T @ tabbidx2g
    mg = sigmoid(s * f64(steep) + f64(bias))
    dmg = f64(pw) * (mg - f64(degree)) * 2.0
    ds = dmg * mg * (1.0 - mg) * f64(steep)
    y = ds + f64(old)
    return y

@@ -1,0 +1,168 @@
+from contextlib import ExitStack
+
+import concourse.mybir as mybir
+from concourse.masks import make_identity
+
+D, T, U, I, J = 512, 1024, 1024, 256, 512
+FLOPS = 2 * D * I * J
+
+F32 = mybir.dt.float32
+BF16 = mybir.dt.bfloat16
+I32 = mybir.dt.int32
+U32 = mybir.dt.uint32
+U16 = mybir.dt.uint16
+U8 = mybir.dt.uint8
+FP8X4 = mybir.dt.float8_e4m3fn_x4
+ACT = mybir.ActivationFunctionType
+ALU = mybir.AluOpType
+
+P = 128
+PACK = 4
+TILES = I // P
+CHUNK = 256
+PER_COLUMN = 16
+
+
+def tile_attend_bpairfit_kernel(tc, taba, tabb_words, tabb_scales, steep, bias, degree, pw, old, offs, offs2, out):
+    nc = tc.nc
+    with ExitStack() as ctx:
+        keep = ctx.enter_context(tc.tile_pool(name="keep", bufs=1))
+        psum = ctx.enter_context(tc.psum_pool(name="psum", bufs=1))
+
+        list_b = keep.tile([P, J // PER_COLUMN], U16, name="list_b")
+        list_a = keep.tile([P, I // PER_COLUMN], U16, name="list_a")
+        nc.sync.dma_start(list_a[:], offs)
+        nc.sync.dma_start(list_b[:], offs2)
+
+        scale_table = keep.tile([P, U], U8, name="scale_table")
+        nc.gpsimd.memset(scale_table[:].bitcast(I32), 0)
+        for q in range(4):
+            nc.scalar.dma_start(
+                out=scale_table[32 * q : 32 * q + 4, :].bitcast(I32),
+                in_=tabb_scales[0, 4 * q : 4 * q + 4, :].bitcast(I32),
+            )
+
+        taba_planes = taba.rearrange("(p t) n -> p t n", t=PACK)
+        planes = []
+        for t in range(PACK):
+            plane = keep.tile([P, T], F32, name="plane%d" % t, tag="plane%d" % t)
+            nc.sync.dma_start(out=plane[:], in_=taba_planes[:, t, :])
+            planes.append(plane[:])
+        word_table = keep.tile([P, U], U32, name="word_table")
+        nc.sync.dma_start(
+            out=word_table[:].bitcast(I32),
+            in_=tabb_words[0].rearrange("p n t -> p (n t)").bitcast(I32),
+        )
+
+        bias_cols = keep.tile([P, PACK], F32, name="bias_cols")
+        pw_cols = keep.tile([P, PACK], F32, name="pw_cols")
+        steep_cols = keep.tile([P, TILES], F32, name="steep_cols")
+        nc.scalar.dma_start(out=bias_cols[:], in_=bias.rearrange("o (p c) -> p (o c)", c=PACK))
+        nc.scalar.dma_start(out=pw_cols[:], in_=pw.rearrange("o (p c) -> p (o c)", c=PACK))
+        ident = keep.tile([P, P], F32, name="ident")
+        make_identity(nc, ident[:])
+        with nc.allow_non_contiguous_dma(reason="one steepness a partition and row tile"):
+            nc.gpsimd.dma_start(out=steep_cols[:], in_=steep.rearrange("(h p) o -> p (h o)", p=P))
+
+        zero = keep.tile([P, 1], F32, name="zero")
+        half = keep.tile([P, 1], F32, name="half")
+        nc.vector.memset(zero[:], 0.0)
+        nc.scalar.activation(half[:], zero[:], ACT.Sigmoid)
+
+        b_scales = keep.tile([P, J], U8, name="b_scales", align_bytes=64)
+        nc.vector.tensor_copy(b_scales[:], scale_table[:].indirect(list_b[:]))
+
+        bias_row = keep.tile([P, J], F32, name="bias_row")
+        pw2_row = keep.tile([P, J], F32, name="pw2_row")
+        for cols, row, factor, name in ((bias_cols, bias_row, 1.0, "bias_bank"), (pw_cols, pw2_row, 2.0, "pw_bank")):
+            bank = psum.tile([P, PACK, P], F32, name=name)
+            for c in range(PACK):
+                nc.tensor.transpose(bank[:, c, :], cols[:, c : c + 1].to_broadcast([P, P]), ident[:])
+            nc.scalar.activation(
+                row[:].rearrange("q (p c) -> q p c", c=PACK),
+                bank[:].rearrange("q c p -> q p c"),
+                ACT.Copy,
+                scale=factor,
+            )
+
+        grouped = keep.tile([P, I * PACK], BF16, name="grouped", align_bytes=64)
+        by_place = grouped[:].rearrange("p (i t) -> p t i", t=PACK)
+        for t in range(PACK):
+            nc.vector.tensor_copy(by_place[:, t, :], planes[t].indirect(list_a[:]))
+
+        degree_sb = keep.tile([P, TILES * J], F32, name="degree_sb", tag="plane0")
+        nc.sync.dma_start(
+            out=degree_sb[:].rearrange("p (h j) -> p h j", h=TILES), in_=degree.rearrange("(h p) j -> p h j", p=P)
+        )
+        old_sb = keep.tile([P, TILES * J], F32, name="old_sb", tag="plane1")
+        nc.sync.dma_start(
+            out=old_sb[:].rearrange("p (h j) -> p h j", h=TILES), in_=old.rearrange("(h p) j -> p h j", p=P)
+        )
+
+        a_words = keep.tile([P, I], U32, name="a_words", align_bytes=64)
+        a_scales = keep.tile([P, I], U8, name="a_scales", align_bytes=64)
+        nc.vector.quantize_mx(out=a_words[:].bitcast(FP8X4), scales=a_scales[:], in_=grouped[:])
+
+        chunks = []
+        for j0 in range(0, J, CHUNK):
+            js = slice(j0, j0 + CHUNK)
+            b_words = keep.tile([P, CHUNK], U32, name="b_words%d" % j0, align_bytes=64)
+            nc.vector.tensor_copy(
+                b_words[:], word_table[:].indirect(list_b[:, js.start // PER_COLUMN : js.stop // PER_COLUMN])
+            )
+            for h in range(TILES):
+                rows = slice(h * P, (h + 1) * P)
+                s = psum.tile([P, CHUNK], F32, name="s%d_%d" % (h, j0))
+                nc.tensor.matmul_mx(
+                    out=s[:],
+                    lhsT=a_words[:, rows].bitcast(FP8X4),
+                    lhsT_scale=a_scales[:, rows],
+                    rhs=b_words[:].bitcast(FP8X4),
+                    rhs_scale=b_scales[:, js],
+                    start=True,
+                    stop=True,
+                )
+                chunks.append((h, js, s))
+
+        def work(name, n):
+            return keep.tile([P, CHUNK], F32, name="%s%d" % (name, n))
+
+        n_chunks = len(chunks)
+        mg = [work("mg", n) for n in range(n_chunks)]
+        sq = [work("sq", n) for n in range(n_chunks)]
+        for n, (h, js, s) in enumerate(chunks):
+            z = work("z", n)
+            nc.vector.scalar_tensor_tensor(z[:], s[:], steep_cols[:, h : h + 1], bias_row[:, js], ALU.mult, ALU.add)
+            nc.scalar.activation(mg[n][:], z[:], ACT.Sigmoid)
+            nc.scalar.activation(sq[n][:], mg[n][:], ACT.Square, bias=half[:], scale=-1.0)
+
+        miss = [work("miss", n) for n in range(n_chunks)]
+        slope = [work("slope", n) for n in range(n_chunks)]
+        ds = [work("ds", n) for n in range(n_chunks)]
+
+        def first(n):
+            h, js, s = chunks[n]
+            both = slice(h * J + js.start, h * J + js.stop)
+            nc.vector.tensor_tensor(miss[n][:], degree_sb[:, both], mg[n][:], ALU.subtract)
+            nc.vector.scalar_tensor_tensor(slope[n][:], sq[n][:], 0.25, pw2_row[:, js], ALU.subtract, ALU.mult)
+
+        def second(n):
+            h, js, s = chunks[n]
+            nc.vector.scalar_tensor_tensor(
+                ds[n][:], miss[n][:], steep_cols[:, h : h + 1], slope[n][:], ALU.mult, ALU.mult
+            )
+
+        def third(n):
+            h, js, s = chunks[n]
+            both = slice(h * J + js.start, h * J + js.stop)
+            result = work("result", n)
+            nc.vector.tensor_tensor(result[:], ds[n][:], old_sb[:, both], ALU.add)
+            nc.sync.dma_start(out=out[h * P : (h + 1) * P, js], in_=result[:])
+
+        for step in range(n_chunks + 2):
+            if step < n_chunks:
+                first(step)
+            if 0 <= step - 2 < n_chunks:
+                third(step - 2)
+            if 0 <= step - 1 < n_chunks:
+                second(step - 1)

@@ -29,10 +29,31 @@ def tile_attend_bpairfit_kernel(tc, taba, tabb_words, tabb_scales, steep, bias, 
         keep = ctx.enter_context(tc.tile_pool(name="keep", bufs=1))
         psum = ctx.enter_context(tc.psum_pool(name="psum", bufs=1))
 
-        list_b = keep.tile([P, J // PER_COLUMN], U16, name="list_b")
         list_a = keep.tile([P, I // PER_COLUMN], U16, name="list_a")
+        list_b = keep.tile([P, J // PER_COLUMN], U16, name="list_b")
+        bias_cols = keep.tile([P, PACK], F32, name="bias_cols")
+        pw_cols = keep.tile([P, PACK], F32, name="pw_cols")
+        word_table = keep.tile([P, U], U32, name="word_table")
+        taba_planes = taba.rearrange("(p t) n -> p t n", t=PACK)
+        planes = []
+
+        def load_plane(t):
+            plane = keep.tile([P, T], F32, name="plane%d" % t, tag="plane%d" % t)
+            nc.sync.dma_start(out=plane[:], in_=taba_planes[:, t, :])
+            planes.append(plane[:])
+
         nc.sync.dma_start(list_a[:], offs)
+        load_plane(0)
         nc.sync.dma_start(list_b[:], offs2)
+        load_plane(1)
+        nc.sync.dma_start(out=bias_cols[:], in_=bias.rearrange("o (p c) -> p (o c)", c=PACK))
+        load_plane(2)
+        nc.sync.dma_start(out=pw_cols[:], in_=pw.rearrange("o (p c) -> p (o c)", c=PACK))
+        load_plane(3)
+        nc.sync.dma_start(
+            out=word_table[:].bitcast(I32),
+            in_=tabb_words[0].rearrange("p n t -> p (n t)").bitcast(I32),
+        )
 
         scale_table = keep.tile([P, U], U8, name="scale_table")
         nc.gpsimd.memset(scale_table[:].bitcast(I32), 0)
@@ -42,31 +63,12 @@ def tile_attend_bpairfit_kernel(tc, taba, tabb_words, tabb_scales, steep, bias, 
                 in_=tabb_scales[0, 4 * q : 4 * q + 4, :].bitcast(I32),
             )
 
-        taba_planes = taba.rearrange("(p t) n -> p t n", t=PACK)
-        planes = []
-        for t in range(PACK):
-            plane = keep.tile([P, T], F32, name="plane%d" % t, tag="plane%d" % t)
-            nc.sync.dma_start(out=plane[:], in_=taba_planes[:, t, :])
-            planes.append(plane[:])
-        word_table = keep.tile([P, U], U32, name="word_table")
-        nc.sync.dma_start(
-            out=word_table[:].bitcast(I32),
-            in_=tabb_words[0].rearrange("p n t -> p (n t)").bitcast(I32),
-        )
-
-        bias_cols = keep.tile([P, PACK], F32, name="bias_cols")
-        pw_cols = keep.tile([P, PACK], F32, name="pw_cols")
-        steep_cols = keep.tile([P, TILES], F32, name="steep_cols")
-        nc.scalar.dma_start(out=bias_cols[:], in_=bias.rearrange("o (p c) -> p (o c)", c=PACK))
-        nc.scalar.dma_start(out=pw_cols[:], in_=pw.rearrange("o (p c) -> p (o c)", c=PACK))
         ident = keep.tile([P, P], F32, name="ident")
         make_identity(nc, ident[:])
-        with nc.allow_non_contiguous_dma(reason="one steepness a partition and row tile"):
-            nc.gpsimd.dma_start(out=steep_cols[:], in_=steep.rearrange("(h p) o -> p (h o)", p=P))
 
         zero = keep.tile([P, 1], F32, name="zero")
         half = keep.tile([P, 1], F32, name="half")
-        nc.vector.memset(zero[:], 0.0)
+        nc.gpsimd.memset(zero[:], 0.0)
         nc.scalar.activation(half[:], zero[:], ACT.Sigmoid)
 
         b_scales = keep.tile([P, J], U8, name="b_scales", align_bytes=64)
@@ -90,11 +92,14 @@ def tile_attend_bpairfit_kernel(tc, taba, tabb_words, tabb_scales, steep, bias, 
         for t in range(PACK):
             nc.vector.tensor_copy(by_place[:, t, :], planes[t].indirect(list_a[:]))
 
-        degree_sb = keep.tile([P, TILES * J], F32, name="degree_sb", tag="plane0")
+        steep_cols = keep.tile([P, TILES], F32, name="steep_cols", tag="plane0")
+        with nc.allow_non_contiguous_dma(reason="one steepness a partition and row tile"):
+            nc.sync.dma_start(out=steep_cols[:], in_=steep.rearrange("(h p) o -> p (h o)", p=P))
+        degree_sb = keep.tile([P, TILES * J], F32, name="degree_sb", tag="plane1")
         nc.sync.dma_start(
             out=degree_sb[:].rearrange("p (h j) -> p h j", h=TILES), in_=degree.rearrange("(h p) j -> p h j", p=P)
         )
-        old_sb = keep.tile([P, TILES * J], F32, name="old_sb", tag="plane1")
+        old_sb = keep.tile([P, TILES * J], F32, name="old_sb", tag="plane2")
         nc.sync.dma_start(
             out=old_sb[:].rearrange("p (h j) -> p h j", h=TILES), in_=old.rearrange("(h p) j -> p h j", p=P)
         )
@@ -162,7 +167,7 @@ def tile_attend_bpairfit_kernel(tc, taba, tabb_words, tabb_scales, steep, bias, 
         for step in range(n_chunks + 2):
             if step < n_chunks:
                 first(step)
-            if 0 <= step - 2 < n_chunks:
-                third(step - 2)
             if 0 <= step - 1 < n_chunks:
                 second(step - 1)
+            if 0 <= step - 2 < n_chunks:
+                third(step - 2)

from contextlib import ExitStack

import concourse.mybir as mybir
from concourse.masks import make_identity

D, T, U, I, J = 512, 1024, 1024, 256, 512
FLOPS = 2 * D * I * J

F32 = mybir.dt.float32
BF16 = mybir.dt.bfloat16
I32 = mybir.dt.int32
U32 = mybir.dt.uint32
U16 = mybir.dt.uint16
U8 = mybir.dt.uint8
FP8X4 = mybir.dt.float8_e4m3fn_x4
ACT = mybir.ActivationFunctionType
ALU = mybir.AluOpType

P = 128
PACK = 4
TILES = I // P
CHUNK = 256
PER_COLUMN = 16


def tile_attend_bpairfit_kernel(tc, taba, tabb_words, tabb_scales, steep, bias, degree, pw, old, offs, offs2, out):
    nc = tc.nc
    with ExitStack() as ctx:
        keep = ctx.enter_context(tc.tile_pool(name="keep", bufs=1))
        psum = ctx.enter_context(tc.psum_pool(name="psum", bufs=1))

        list_a = keep.tile([P, I // PER_COLUMN], U16, name="list_a")
        list_b = keep.tile([P, J // PER_COLUMN], U16, name="list_b")
        bias_cols = keep.tile([P, PACK], F32, name="bias_cols")
        pw_cols = keep.tile([P, PACK], F32, name="pw_cols")
        word_table = keep.tile([P, U], U32, name="word_table")
        taba_planes = taba.rearrange("(p t) n -> p t n", t=PACK)
        planes = []

        def load_plane(t):
            plane = keep.tile([P, T], F32, name="plane%d" % t, tag="plane%d" % t)
            nc.sync.dma_start(out=plane[:], in_=taba_planes[:, t, :])
            planes.append(plane[:])

        nc.sync.dma_start(list_a[:], offs)
        load_plane(0)
        nc.sync.dma_start(list_b[:], offs2)
        load_plane(1)
        nc.sync.dma_start(out=bias_cols[:], in_=bias.rearrange("o (p c) -> p (o c)", c=PACK))
        load_plane(2)
        nc.sync.dma_start(out=pw_cols[:], in_=pw.rearrange("o (p c) -> p (o c)", c=PACK))
        load_plane(3)
        nc.sync.dma_start(
            out=word_table[:].bitcast(I32),
            in_=tabb_words[0].rearrange("p n t -> p (n t)").bitcast(I32),
        )

        scale_table = keep.tile([P, U], U8, name="scale_table")
        nc.gpsimd.memset(scale_table[:].bitcast(I32), 0)
        for q in range(4):
            nc.scalar.dma_start(
                out=scale_table[32 * q : 32 * q + 4, :].bitcast(I32),
                in_=tabb_scales[0, 4 * q : 4 * q + 4, :].bitcast(I32),
            )

        ident = keep.tile([P, P], F32, name="ident")
        make_identity(nc, ident[:])

        zero = keep.tile([P, 1], F32, name="zero")
        half = keep.tile([P, 1], F32, name="half")
        nc.gpsimd.memset(zero[:], 0.0)
        nc.scalar.activation(half[:], zero[:], ACT.Sigmoid)

        b_scales = keep.tile([P, J], U8, name="b_scales", align_bytes=64)
        nc.vector.tensor_copy(b_scales[:], scale_table[:].indirect(list_b[:]))

        bias_row = keep.tile([P, J], F32, name="bias_row")
        pw2_row = keep.tile([P, J], F32, name="pw2_row")
        for cols, row, factor, name in ((bias_cols, bias_row, 1.0, "bias_bank"), (pw_cols, pw2_row, 2.0, "pw_bank")):
            bank = psum.tile([P, PACK, P], F32, name=name)
            for c in range(PACK):
                nc.tensor.transpose(bank[:, c, :], cols[:, c : c + 1].to_broadcast([P, P]), ident[:])
            nc.scalar.activation(
                row[:].rearrange("q (p c) -> q p c", c=PACK),
                bank[:].rearrange("q c p -> q p c"),
                ACT.Copy,
                scale=factor,
            )

        grouped = keep.tile([P, I * PACK], BF16, name="grouped", align_bytes=64)
        by_place = grouped[:].rearrange("p (i t) -> p t i", t=PACK)
        for t in range(PACK):
            nc.vector.tensor_copy(by_place[:, t, :], planes[t].indirect(list_a[:]))

        steep_cols = keep.tile([P, TILES], F32, name="steep_cols", tag="plane0")
        with nc.allow_non_contiguous_dma(reason="one steepness a partition and row tile"):
            nc.sync.dma_start(out=steep_cols[:], in_=steep.rearrange("(h p) o -> p (h o)", p=P))
        degree_sb = keep.tile([P, TILES * J], F32, name="degree_sb", tag="plane1")
        nc.sync.dma_start(
            out=degree_sb[:].rearrange("p (h j) -> p h j", h=TILES), in_=degree.rearrange("(h p) j -> p h j", p=P)
        )
        old_sb = keep.tile([P, TILES * J], F32, name="old_sb", tag="plane2")
        nc.sync.dma_start(
            out=old_sb[:].rearrange("p (h j) -> p h j", h=TILES), in_=old.rearrange("(h p) j -> p h j", p=P)
        )

        a_words = keep.tile([P, I], U32, name="a_words", align_bytes=64)
        a_scales = keep.tile([P, I], U8, name="a_scales", align_bytes=64)
        nc.vector.quantize_mx(out=a_words[:].bitcast(FP8X4), scales=a_scales[:], in_=grouped[:])

        chunks = []
        for j0 in range(0, J, CHUNK):
            js = slice(j0, j0 + CHUNK)
            b_words = keep.tile([P, CHUNK], U32, name="b_words%d" % j0, align_bytes=64)
            nc.vector.tensor_copy(
                b_words[:], word_table[:].indirect(list_b[:, js.start // PER_COLUMN : js.stop // PER_COLUMN])
            )
            for h in range(TILES):
                rows = slice(h * P, (h + 1) * P)
                s = psum.tile([P, CHUNK], F32, name="s%d_%d" % (h, j0))
                nc.tensor.matmul_mx(
                    out=s[:],
                    lhsT=a_words[:, rows].bitcast(FP8X4),
                    lhsT_scale=a_scales[:, rows],
                    rhs=b_words[:].bitcast(FP8X4),
                    rhs_scale=b_scales[:, js],
                    start=True,
                    stop=True,
                )
                chunks.append((h, js, s))

        def work(name, n):
            return keep.tile([P, CHUNK], F32, name="%s%d" % (name, n))

        n_chunks = len(chunks)
        mg = [work("mg", n) for n in range(n_chunks)]
        sq = [work("sq", n) for n in range(n_chunks)]
        for n, (h, js, s) in enumerate(chunks):
            z = work("z", n)
            nc.vector.scalar_tensor_tensor(z[:], s[:], steep_cols[:, h : h + 1], bias_row[:, js], ALU.mult, ALU.add)
            nc.scalar.activation(mg[n][:], z[:], ACT.Sigmoid)
            nc.scalar.activation(sq[n][:], mg[n][:], ACT.Square, bias=half[:], scale=-1.0)

        miss = [work("miss", n) for n in range(n_chunks)]
        slope = [work("slope", n) for n in range(n_chunks)]
        ds = [work("ds", n) for n in range(n_chunks)]

        def first(n):
            h, js, s = chunks[n]
            both = slice(h * J + js.start, h * J + js.stop)
            nc.vector.tensor_tensor(miss[n][:], degree_sb[:, both], mg[n][:], ALU.subtract)
            nc.vector.scalar_tensor_tensor(slope[n][:], sq[n][:], 0.25, pw2_row[:, js], ALU.subtract, ALU.mult)

        def second(n):
            h, js, s = chunks[n]
            nc.vector.scalar_tensor_tensor(
                ds[n][:], miss[n][:], steep_cols[:, h : h + 1], slope[n][:], ALU.mult, ALU.mult
            )

        def third(n):
            h, js, s = chunks[n]
            both = slice(h * J + js.start, h * J + js.stop)
            result = work("result", n)
            nc.vector.tensor_tensor(result[:], ds[n][:], old_sb[:, both], ALU.add)
            nc.sync.dma_start(out=out[h * P : (h + 1) * P, js], in_=result[:])

        for step in range(n_chunks + 2):
            if step < n_chunks:
                first(step)
            if 0 <= step - 1 < n_chunks:
                second(step - 1)
            if 0 <= step - 2 < n_chunks:
                third(step - 2)
